import numpy as np
import ml_dtypes

BF16 = ml_dtypes.bfloat16


def bf(x):
    return np.asarray(x, np.float32).astype(BF16)


def f32(x):
    return np.asarray(x, np.float32)


def f64(x):
    return np.asarray(x).astype(np.float64)


def striped(idx):
    return np.tile(idx.reshape(-1, 16).T, (8, 1))


S, K, M, N, E, Q = 256, 256, 512, 128, 2, 64


def setup_inputs():
    return {"base": bf(np.random.standard_normal((M, S))), "x": bf(np.random.standard_normal((K, N))), "w": bf(np.random.standard_normal((E, K, M)) / np.sqrt(K)), "offs": striped(np.random.permutation(S)[:N])}


def reference(base, x, w, offs):
    idx = offs[:16].T.reshape(-1)
    z = f64(base).copy()
    for e in range(E):
        z[:, idx[e * Q : (e + 1) * Q]] += f64(w)[e].T @ f64(x)[:, e * Q : (e + 1) * Q]
    return z

@@ -1,0 +1,54 @@
+import concourse.mybir as mybir
+from concourse.masks import make_identity
+
+P = 128
+S, K, M, N = 256, 256, 512, 128
+E = 2
+Q = N // E
+A, B = M // P, K // P
+BF16, F32, U16 = mybir.dt.bfloat16, mybir.dt.float32, mybir.dt.uint16
+
+FLOPS = 2 * K * M * N
+
+
+def tile_scatter_matmul_kernel(tc, base, x, w, offs, out):
+    nc = tc.nc
+    with (
+        tc.tile_pool(name="held", bufs=1) as held,
+        tc.psum_pool(name="psum", bufs=1) as psum,
+    ):
+        offsets = held.tile([P, N // 16], U16, name="offsets")
+        base_sb = held.tile([P, A, S], BF16, name="base_sb")
+        x_sb = held.tile([P, B, N], BF16, name="x_sb")
+        w_sb = held.tile([P, E, B, M], BF16, name="w_sb")
+        ident = held.tile([P, P], BF16, name="ident")
+        z_sb = held.tile([P, A, S], F32, name="z_sb")
+        windows = [psum.tile([P, S], F32, name=f"window{a}") for a in range(A)]
+
+        nc.sync.dma_start(base_sb[:], base.rearrange("(a p) s -> p a s", p=P))
+        nc.sync.dma_start(offsets[:], offs)
+        nc.sync.dma_start(x_sb[:], x.rearrange("(p b) n -> p b n", b=B))
+        nc.sync.dma_start(w_sb[:], w.rearrange("e (p b) m -> p e b m", b=B))
+        make_identity(nc, ident[:])
+
+        for a in range(A):
+            nc.tensor.matmul(windows[a][:], ident[:], base_sb[:, a, :], start=True, stop=False)
+
+        for a in range(A):
+            for e in range(E):
+                piece = offsets[:, e * (Q // 16) : (e + 1) * (Q // 16)]
+                for b in range(B):
+                    nc.tensor.matmul(
+                        windows[a][:].indirect(piece),
+                        w_sb[:, e, b, a * P : (a + 1) * P],
+                        x_sb[:, b, e * Q : (e + 1) * Q],
+                        start=False,
+                        stop=(e == E - 1 and b == B - 1),
+                    )
+
+        for a in range(A):
+            if a % 2 == 0:
+                nc.vector.tensor_copy(z_sb[:, a, :], windows[a][:])
+            else:
+                nc.scalar.copy(z_sb[:, a, :], windows[a][:])
+            nc.sync.dma_start(out[a * P : (a + 1) * P, :], z_sb[:, a, :])

@@ -5,6 +5,7 @@ P = 128
 S, K, M, N = 256, 256, 512, 128
 E = 2
 Q = N // E
+WARM_UP = 5
 A, B = M // P, K // P
 BF16, F32, U16 = mybir.dt.bfloat16, mybir.dt.float32, mybir.dt.uint16
 
@@ -22,14 +23,20 @@ def tile_scatter_matmul_kernel(tc, base, x, w, offs, out):
         x_sb = held.tile([P, B, N], BF16, name="x_sb")
         w_sb = held.tile([P, E, B, M], BF16, name="w_sb")
         ident = held.tile([P, P], BF16, name="ident")
+        zeros = held.tile([P, 512], BF16, name="zeros")
         z_sb = held.tile([P, A, S], F32, name="z_sb")
         windows = [psum.tile([P, S], F32, name=f"window{a}") for a in range(A)]
+        idle_bank = psum.tile([P, 512], F32, name="idle_bank")
 
         nc.sync.dma_start(base_sb[:], base.rearrange("(a p) s -> p a s", p=P))
         nc.sync.dma_start(offsets[:], offs)
         nc.sync.dma_start(x_sb[:], x.rearrange("(p b) n -> p b n", b=B))
         nc.sync.dma_start(w_sb[:], w.rearrange("e (p b) m -> p e b m", b=B))
         make_identity(nc, ident[:])
+
+        nc.vector.memset(zeros[:], 0.0)
+        for i in range(WARM_UP):
+            nc.tensor.matmul(idle_bank[:], zeros[:, :P], zeros[:], start=True, stop=True)
 
         for a in range(A):
             nc.tensor.matmul(windows[a][:], ident[:], base_sb[:, a, :], start=True, stop=False)

@@ -5,7 +5,7 @@ P = 128
 S, K, M, N = 256, 256, 512, 128
 E = 2
 Q = N // E
-WARM_UP = 5
+WARM_UP = 7
 A, B = M // P, K // P
 BF16, F32, U16 = mybir.dt.bfloat16, mybir.dt.float32, mybir.dt.uint16
 
@@ -23,10 +23,10 @@ def tile_scatter_matmul_kernel(tc, base, x, w, offs, out):
         x_sb = held.tile([P, B, N], BF16, name="x_sb")
         w_sb = held.tile([P, E, B, M], BF16, name="w_sb")
         ident = held.tile([P, P], BF16, name="ident")
-        zeros = held.tile([P, 512], BF16, name="zeros")
+        zeros = held.tile([P, S], BF16, name="zeros")
         z_sb = held.tile([P, A, S], F32, name="z_sb")
         windows = [psum.tile([P, S], F32, name=f"window{a}") for a in range(A)]
-        idle_bank = psum.tile([P, 512], F32, name="idle_bank")
+        idle_bank = psum.tile([P, S], F32, name="idle_bank")
 
         nc.sync.dma_start(base_sb[:], base.rearrange("(a p) s -> p a s", p=P))
         nc.sync.dma_start(offsets[:], offs)

import concourse.mybir as mybir
from concourse.masks import make_identity

P = 128
S, K, M, N = 256, 256, 512, 128
E = 2
Q = N // E
WARM_UP = 7
A, B = M // P, K // P
BF16, F32, U16 = mybir.dt.bfloat16, mybir.dt.float32, mybir.dt.uint16

FLOPS = 2 * K * M * N


def tile_scatter_matmul_kernel(tc, base, x, w, offs, out):
    nc = tc.nc
    with (
        tc.tile_pool(name="held", bufs=1) as held,
        tc.psum_pool(name="psum", bufs=1) as psum,
    ):
        offsets = held.tile([P, N // 16], U16, name="offsets")
        base_sb = held.tile([P, A, S], BF16, name="base_sb")
        x_sb = held.tile([P, B, N], BF16, name="x_sb")
        w_sb = held.tile([P, E, B, M], BF16, name="w_sb")
        ident = held.tile([P, P], BF16, name="ident")
        zeros = held.tile([P, S], BF16, name="zeros")
        z_sb = held.tile([P, A, S], F32, name="z_sb")
        windows = [psum.tile([P, S], F32, name=f"window{a}") for a in range(A)]
        idle_bank = psum.tile([P, S], F32, name="idle_bank")

        nc.sync.dma_start(base_sb[:], base.rearrange("(a p) s -> p a s", p=P))
        nc.sync.dma_start(offsets[:], offs)
        nc.sync.dma_start(x_sb[:], x.rearrange("(p b) n -> p b n", b=B))
        nc.sync.dma_start(w_sb[:], w.rearrange("e (p b) m -> p e b m", b=B))
        make_identity(nc, ident[:])

        nc.vector.memset(zeros[:], 0.0)
        for i in range(WARM_UP):
            nc.tensor.matmul(idle_bank[:], zeros[:, :P], zeros[:], start=True, stop=True)

        for a in range(A):
            nc.tensor.matmul(windows[a][:], ident[:], base_sb[:, a, :], start=True, stop=False)

        for a in range(A):
            for e in range(E):
                piece = offsets[:, e * (Q // 16) : (e + 1) * (Q // 16)]
                for b in range(B):
                    nc.tensor.matmul(
                        windows[a][:].indirect(piece),
                        w_sb[:, e, b, a * P : (a + 1) * P],
                        x_sb[:, b, e * Q : (e + 1) * Q],
                        start=False,
                        stop=(e == E - 1 and b == B - 1),
                    )

        for a in range(A):
            if a % 2 == 0:
                nc.vector.tensor_copy(z_sb[:, a, :], windows[a][:])
            else:
                nc.scalar.copy(z_sb[:, a, :], windows[a][:])
            nc.sync.dma_start(out[a * P : (a + 1) * P, :], z_sb[:, a, :])
